import numpy as np
import ml_dtypes


def mxq(x, axis, fmt="e4m3"):
    dtype, down = {"e4m3": (ml_dtypes.float8_e4m3fn, 7), "e5m2": (ml_dtypes.float8_e5m2, 14)}[fmt]
    v = np.moveaxis(np.asarray(x, np.float32).astype(ml_dtypes.bfloat16).astype(np.float64), axis, -1)
    blocks = v.reshape(v.shape[:-1] + (-1, 32))
    amax = np.abs(blocks).max(-1, keepdims=True)
    byte = np.maximum(np.where(amax > 0, np.frexp(amax)[1] - 1 + 127, 0) - down, 1)
    scale = np.exp2(byte - 127.0)
    codes = (blocks / scale).astype(np.float32).astype(dtype).astype(np.float64)
    return np.moveaxis((codes * scale).reshape(v.shape), -1, axis)


WIDE = False


def mx_kscale(k):
    if not WIDE:
        return np.ones(k)
    levels = np.array([10, -10, 5, -5, 0])
    if k % 512:
        return np.exp2(np.random.permutation(np.resize(levels, k // 32))).repeat(32)
    a = np.empty((k // 512, 16))
    for p in range(k // 512):
        a[p, :8] = np.random.permutation(np.resize(levels, 8))
        for g in range(8):
            far = levels[np.abs(levels - a[p, g]) >= 10]
            a[p, g + 8] = far[np.random.randint(len(far))]
    return np.exp2(a.ravel()).repeat(32)


def f64(x):
    return np.asarray(x).astype(np.float64)


def striped8(idx):
    return np.concatenate([v.reshape(-1, 16).T for v in idx]).astype(np.uint16)


def unstriped8(offs):
    return np.stack([offs[16 * g:16 * g + 16].T.reshape(-1) for g in range(8)]).astype(np.int64)


K, M, T, S = 2048, 512, 1024, 512


def setup_inputs():
    n = np.random.standard_normal
    s = mx_kscale(K)[:, None]
    return {
        "xT": (n((K, T)) * s).astype(np.float32),
        "w": (n((K, M)) / np.sqrt(K) / s).astype(np.float32),
        "wgt": np.repeat(np.random.uniform(0.5, 2.0, (8, S)), 16, axis=0).astype(np.float32),
        "offs": striped8(np.stack([np.random.permutation(T)[:S] for _ in range(8)])),
    }


def reference(xT, w, wgt, offs):
    idx = unstriped8(offs)
    group = np.arange(K) % 512 // 64
    xg = f64(wgt)[np.arange(K) // 4 % 128] * f64(xT)[np.arange(K)[:, None], idx[group]]
    xT_ = mxq(xg, 0, "e4m3")
    w_ = mxq(f64(w), 0, "e4m3")
    y = w_.T @ xT_
    return y

@@ -1,0 +1,174 @@
+from contextlib import ExitStack
+
+import concourse.mybir as mybir
+
+K, M, T, S = 2048, 512, 1024, 512
+FLOPS = 2 * K * M * S
+
+F32 = mybir.dt.float32
+BF16 = mybir.dt.bfloat16
+U32 = mybir.dt.uint32
+U16 = mybir.dt.uint16
+U8 = mybir.dt.uint8
+FP8X4 = mybir.dt.float8_e4m3fn_x4
+MULT = mybir.AluOpType.mult
+
+P = 128
+PACK = 4
+PASSES = K // (P * PACK)
+HALF = S // 2
+
+
+def tile_list_heads_none_kernel(tc, xT, w, wgt, offs, out):
+    nc = tc.nc
+    with ExitStack() as ctx:
+        keep = ctx.enter_context(tc.tile_pool(name="keep", bufs=1))
+        stage = ctx.enter_context(tc.tile_pool(name="stage", bufs=3))
+        psum = ctx.enter_context(tc.psum_pool(name="psum", bufs=1))
+
+        offsets = keep.tile([P, S // 16], U16, name="offsets")
+        weight = keep.tile([P, S], F32, name="weight")
+        planes = [[keep.tile([P, T], F32, name=f"x{a}_{t}", align_bytes=64) for t in range(PACK)] for a in range(PASSES)]
+        w_raw = [keep.tile([P, PACK, M], F32, name=f"w{a}") for a in range(PASSES)]
+        x_scales = keep.tile([P, PASSES, S], U8, name="x_scales", align_bytes=64)
+        w_scales = keep.tile([P, PASSES, M], U8, name="w_scales", align_bytes=64)
+        acc = [psum.tile([P, S], F32, name=f"acc{m}") for m in range(M // P)]
+
+        xv = xT.rearrange("(a p t) s -> a t p s", p=P, t=PACK)
+        wv = w.rearrange("(a p t) n -> a p t n", p=P, t=PACK)
+
+        def load_x(a):
+            for t in range(PACK):
+                nc.sync.dma_start(out=planes[a][t][:], in_=xv[a, t])
+
+        def load_w(a, lo, hi):
+            nc.sync.dma_start(out=w_raw[a][:, :, lo:hi], in_=wv[a, :, :, lo:hi])
+
+        nc.sync.dma_start(offsets[:], offs)
+        nc.sync.dma_start(out=weight[:], in_=wgt)
+        load_x(0)
+        load_x(1)
+        load_w(0, 0, M)
+        load_x(2)
+        load_w(1, 0, M)
+        load_w(2, 0, M)
+        load_x(3)
+        load_w(3, 0, 256)
+        load_w(3, 256, 512)
+
+        picked, xb, wb, x_codes, w_codes = {}, {}, {}, {}, {}
+
+        def gather(a, t):
+            if t == 0:
+                picked[a] = stage.tile([P, PACK, S], F32, name="picked")
+            for h in range(2):
+                cols = slice(h * HALF, (h + 1) * HALF)
+                nc.vector.tensor_tensor(
+                    picked[a][:, t, cols],
+                    planes[a][t][:].indirect(offsets[:, h * HALF // 16 : (h + 1) * HALF // 16]),
+                    weight[:, cols],
+                    MULT,
+                )
+
+        def interleave(copy, dst, src, lo, hi):
+            copy(
+                out=dst[:, lo:hi, :].rearrange("p (c i) t -> p c t i", i=4),
+                in_=src[:, :, lo:hi].rearrange("p t (c i) -> p c t i", i=4),
+            )
+
+        def quantize(words, scales, src):
+            nc.vector.quantize_mx(out=words.bitcast(FP8X4), scales=scales, in_=src.rearrange("p w t -> p (w t)"))
+
+        def x_tile(a):
+            xb[a] = stage.tile([P, S, PACK], BF16, name="xb", align_bytes=64)
+
+        def w_tile(a, name):
+            wb[a] = keep.tile([P, M, PACK], BF16, name=name, align_bytes=64)
+
+        def codes(store, a, name):
+            store[a] = keep.tile([P, M], U32, name=name, align_bytes=64)
+
+        def copy_x(a):
+            x_tile(a)
+            for h in range(2):
+                interleave(nc.scalar.copy, xb[a], picked[a], h * HALF, (h + 1) * HALF)
+
+        def quant_x(a):
+            quantize(x_codes[a][:], x_scales[:, a, :], xb[a][:])
+
+        def quant_w(a, lo, hi):
+            quantize(w_codes[a][:, lo:hi], w_scales[:, a, lo:hi], wb[a][:, lo:hi, :])
+
+        def matmul(a, m):
+            cols = slice(m * P, (m + 1) * P)
+            nc.tensor.matmul_mx(
+                out=acc[m][:],
+                lhsT=w_codes[a][:, cols].bitcast(FP8X4),
+                lhsT_scale=w_scales[:, a, cols],
+                rhs=x_codes[a][:].bitcast(FP8X4),
+                rhs_scale=x_scales[:, a, :],
+                start=(a == 0),
+                stop=(a == PASSES - 1),
+            )
+
+        def matmuls(a):
+            for m in range(M // P):
+                matmul(a, m)
+
+        for t in range(PACK):
+            gather(0, t)
+        copy_x(0)
+        for t in range(PACK):
+            gather(1, t)
+        codes(x_codes, 0, "x1_3")
+        quant_x(0)
+        w_tile(0, "wb0")
+        interleave(nc.scalar.copy, wb[0], w_raw[0], 0, M)
+        copy_x(1)
+        for t in range(PACK):
+            gather(2, t)
+            if t == 2:
+                codes(w_codes, 0, "x2_2")
+                quant_w(0, 0, M)
+        codes(x_codes, 1, "x2_3")
+        quant_x(1)
+        matmuls(0)
+        x_tile(2)
+        interleave(nc.scalar.copy, xb[2], picked[2], 0, HALF)
+        interleave(nc.vector.tensor_copy, xb[2], picked[2], HALF, S)
+        w_tile(1, "x2_0")
+        interleave(nc.scalar.copy, wb[1], w_raw[1], 0, 256)
+        interleave(nc.vector.tensor_copy, wb[1], w_raw[1], 256, M)
+        codes(x_codes, 2, "x_codes2")
+        quant_x(2)
+        codes(w_codes, 1, "w_codes1")
+        quant_w(1, 0, M)
+        matmuls(1)
+        w_tile(2, "wb2")
+        interleave(nc.scalar.copy, wb[2], w_raw[2], 0, M)
+        for t in range(PACK):
+            gather(3, t)
+            if t == 1:
+                codes(w_codes, 2, "x3_1")
+                quant_w(2, 0, M)
+                matmuls(2)
+        w_tile(3, "wb3")
+        interleave(nc.scalar.copy, wb[3], w_raw[3], 0, 256)
+        x_tile(3)
+        interleave(nc.scalar.copy, xb[3], picked[3], 0, HALF)
+        interleave(nc.vector.tensor_copy, xb[3], picked[3], HALF, S)
+        codes(w_codes, 3, "x3_3")
+        quant_w(3, 0, 256)
+        codes(x_codes, 3, "x_codes3")
+        quant_x(3)
+        interleave(nc.scalar.copy, wb[3], w_raw[3], 256, 384)
+        interleave(nc.vector.tensor_copy, wb[3], w_raw[3], 384, M)
+        quant_w(3, 256, M)
+        for m in range(M // P):
+            matmul(3, m)
+            result = keep.tile([P, S], F32, name=f"result{m}")
+            if m % 2:
+                nc.scalar.copy(out=result[:], in_=acc[m][:])
+            else:
+                nc.vector.tensor_copy(out=result[:], in_=acc[m][:])
+            nc.sync.dma_start(out=out[m * P : (m + 1) * P, :], in_=result[:])

@@ -17,6 +17,7 @@ P = 128
 PACK = 4
 PASSES = K // (P * PACK)
 HALF = S // 2
+assert M == S
 
 
 def tile_list_heads_none_kernel(tc, xT, w, wgt, offs, out):
@@ -30,33 +31,35 @@ def tile_list_heads_none_kernel(tc, xT, w, wgt, offs, out):
         weight = keep.tile([P, S], F32, name="weight")
         planes = [[keep.tile([P, T], F32, name=f"x{a}_{t}", align_bytes=64) for t in range(PACK)] for a in range(PASSES)]
         w_raw = [keep.tile([P, PACK, M], F32, name=f"w{a}") for a in range(PASSES)]
-        x_scales = keep.tile([P, PASSES, S], U8, name="x_scales", align_bytes=64)
-        w_scales = keep.tile([P, PASSES, M], U8, name="w_scales", align_bytes=64)
         acc = [psum.tile([P, S], F32, name=f"acc{m}") for m in range(M // P)]
 
         xv = xT.rearrange("(a p t) s -> a t p s", p=P, t=PACK)
         wv = w.rearrange("(a p t) n -> a p t n", p=P, t=PACK)
 
-        def load_x(a):
-            for t in range(PACK):
-                nc.sync.dma_start(out=planes[a][t][:], in_=xv[a, t])
+        def load_x(a, t):
+            nc.sync.dma_start(out=planes[a][t][:], in_=xv[a, t])
 
-        def load_w(a, lo, hi):
-            nc.sync.dma_start(out=w_raw[a][:, :, lo:hi], in_=wv[a, :, :, lo:hi])
+        def load_w(a):
+            nc.sync.dma_start(out=w_raw[a][:], in_=wv[a])
 
         nc.sync.dma_start(offsets[:], offs)
-        nc.sync.dma_start(out=weight[:], in_=wgt)
-        load_x(0)
-        load_x(1)
-        load_w(0, 0, M)
-        load_x(2)
-        load_w(1, 0, M)
-        load_w(2, 0, M)
-        load_x(3)
-        load_w(3, 0, 256)
-        load_w(3, 256, 512)
+        nc.sync.dma_start(out=weight[:, :HALF], in_=wgt[:, :HALF])
+        load_x(0, 0)
+        nc.sync.dma_start(out=weight[:, HALF:], in_=wgt[:, HALF:])
+        for a, t in ((0, 1), (0, 2), (0, 3), (1, 0), (1, 1), (1, 2), (1, 3), (2, 0), (2, 1)):
+            load_x(a, t)
+        load_w(0)
+        load_x(2, 2)
+        load_x(2, 3)
+        load_x(3, 0)
+        load_w(1)
+        load_x(3, 1)
+        load_x(3, 2)
+        load_w(2)
+        load_x(3, 3)
+        load_w(3)
 
-        picked, xb, wb, x_codes, w_codes = {}, {}, {}, {}, {}
+        picked, rounded, quantized = {}, {}, {}
 
         def gather(a, t):
             if t == 0:
@@ -70,43 +73,44 @@ def tile_list_heads_none_kernel(tc, xT, w, wgt, offs, out):
                     MULT,
                 )
 
-        def interleave(copy, dst, src, lo, hi):
+        def open_group(label, keys):
+            tile = keep.tile([P, len(keys), S, PACK], BF16, name=f"rounded_{label}", align_bytes=64)
+            for i, key in enumerate(keys):
+                rounded[key] = tile[:, i]
+            return tile
+
+        def interleave(copy, key, lo, hi):
+            side, a = key
+            src = picked[a] if side == "x" else w_raw[a]
             copy(
-                out=dst[:, lo:hi, :].rearrange("p (c i) t -> p c t i", i=4),
+                out=rounded[key][:, lo:hi, :].rearrange("p (c i) t -> p c t i", i=4),
                 in_=src[:, :, lo:hi].rearrange("p t (c i) -> p c t i", i=4),
             )
 
-        def quantize(words, scales, src):
-            nc.vector.quantize_mx(out=words.bitcast(FP8X4), scales=scales, in_=src.rearrange("p w t -> p (w t)"))
-
-        def x_tile(a):
-            xb[a] = stage.tile([P, S, PACK], BF16, name="xb", align_bytes=64)
-
-        def w_tile(a, name):
-            wb[a] = keep.tile([P, M, PACK], BF16, name=name, align_bytes=64)
-
-        def codes(store, a, name):
-            store[a] = keep.tile([P, M], U32, name=name, align_bytes=64)
-
-        def copy_x(a):
-            x_tile(a)
-            for h in range(2):
-                interleave(nc.scalar.copy, xb[a], picked[a], h * HALF, (h + 1) * HALF)
-
-        def quant_x(a):
-            quantize(x_codes[a][:], x_scales[:, a, :], xb[a][:])
-
-        def quant_w(a, lo, hi):
-            quantize(w_codes[a][:, lo:hi], w_scales[:, a, lo:hi], wb[a][:, lo:hi, :])
+        def quantize(tile, keys, label, slot, parts=1):
+            words = keep.tile([P, len(keys), S], U32, name=slot, align_bytes=64)
+            scales = keep.tile([P, len(keys), S], U8, name=f"scales_{label}", align_bytes=64)
+            columns = len(keys) * S
+            for part in range(parts):
+                cols = slice(part * columns // parts, (part + 1) * columns // parts)
+                nc.vector.quantize_mx(
+                    out=words[:].rearrange("p k s -> p (k s)")[:, cols].bitcast(FP8X4),
+                    scales=scales[:].rearrange("p k s -> p (k s)")[:, cols],
+                    in_=tile[:].rearrange("p k s t -> p (k s) t")[:, cols, :].rearrange("p c t -> p (c t)"),
+                )
+            for i, key in enumerate(keys):
+                quantized[key] = (words[:, i], scales[:, i])
 
         def matmul(a, m):
             cols = slice(m * P, (m + 1) * P)
+            w_words, w_scales = quantized["w", a]
+            x_words, x_scales = quantized["x", a]
             nc.tensor.matmul_mx(
                 out=acc[m][:],
-                lhsT=w_codes[a][:, cols].bitcast(FP8X4),
-                lhsT_scale=w_scales[:, a, cols],
-                rhs=x_codes[a][:].bitcast(FP8X4),
-                rhs_scale=x_scales[:, a, :],
+                lhsT=w_words[:, cols].bitcast(FP8X4),
+                lhsT_scale=w_scales[:, cols],
+                rhs=x_words.bitcast(FP8X4),
+                rhs_scale=x_scales,
                 start=(a == 0),
                 stop=(a == PASSES - 1),
             )
@@ -115,55 +119,47 @@ def tile_list_heads_none_kernel(tc, xT, w, wgt, offs, out):
             for m in range(M // P):
                 matmul(a, m)
 
+        scalar, vector = nc.scalar.copy, nc.vector.tensor_copy
         for t in range(PACK):
             gather(0, t)
-        copy_x(0)
-        for t in range(PACK):
-            gather(1, t)
-        codes(x_codes, 0, "x1_3")
-        quant_x(0)
-        w_tile(0, "wb0")
-        interleave(nc.scalar.copy, wb[0], w_raw[0], 0, M)
-        copy_x(1)
+        x0 = open_group("x0", [("x", 0)])
+        interleave(scalar, ("x", 0), 0, HALF)
+        interleave(scalar, ("x", 0), HALF, S)
+        gather(1, 0)
+        gather(1, 1)
+        gather(1, 2)
+        quantize(x0, [("x", 0)], "x0", "x1_1")
+        gather(1, 3)
+        x1w0 = open_group("x1w0", [("x", 1), ("w", 0)])
+        interleave(scalar, ("x", 1), 0, HALF)
+        interleave(scalar, ("x", 1), HALF, S)
+        interleave(scalar, ("w", 0), 0, M)
         for t in range(PACK):
             gather(2, t)
-            if t == 2:
-                codes(w_codes, 0, "x2_2")
-                quant_w(0, 0, M)
-        codes(x_codes, 1, "x2_3")
-        quant_x(1)
+        quantize(x1w0, [("x", 1), ("w", 0)], "x1w0", "x2_2")
         matmuls(0)
-        x_tile(2)
-        interleave(nc.scalar.copy, xb[2], picked[2], 0, HALF)
-        interleave(nc.vector.tensor_copy, xb[2], picked[2], HALF, S)
-        w_tile(1, "x2_0")
-        interleave(nc.scalar.copy, wb[1], w_raw[1], 0, 256)
-        interleave(nc.vector.tensor_copy, wb[1], w_raw[1], 256, M)
-        codes(x_codes, 2, "x_codes2")
-        quant_x(2)
-        codes(w_codes, 1, "w_codes1")
-        quant_w(1, 0, M)
+        x2w1 = open_group("x2w1", [("x", 2), ("w", 1)])
+        interleave(scalar, ("x", 2), 0, HALF)
+        interleave(scalar, ("x", 2), HALF, S)
+        interleave(scalar, ("w", 1), 0, M)
+        gather(3, 0)
+        gather(3, 1)
+        gather(3, 2)
+        quantize(x2w1, [("x", 2), ("w", 1)], "x2w1", "x3_2")
         matmuls(1)
-        w_tile(2, "wb2")
-        interleave(nc.scalar.copy, wb[2], w_raw[2], 0, M)
-        for t in range(PACK):
-            gather(3, t)
-            if t == 1:
-                codes(w_codes, 2, "x3_1")
-                quant_w(2, 0, M)
-                matmuls(2)
-        w_tile(3, "wb3")
-        interleave(nc.scalar.copy, wb[3], w_raw[3], 0, 256)
-        x_tile(3)
-        interleave(nc.scalar.copy, xb[3], picked[3], 0, HALF)
-        interleave(nc.vector.tensor_copy, xb[3], picked[3], HALF, S)
-        codes(w_codes, 3, "x3_3")
-        quant_w(3, 0, 256)
-        codes(x_codes, 3, "x_codes3")
-        quant_x(3)
-        interleave(nc.scalar.copy, wb[3], w_raw[3], 256, 384)
-        interleave(nc.vector.tensor_copy, wb[3], w_raw[3], 384, M)
-        quant_w(3, 256, M)
+        w2 = open_group("w2", [("w", 2)])
+        interleave(scalar, ("w", 2), 0, M)
+        gather(3, 3)
+        quantize(w2, [("w", 2)], "w2", "x3_3")
+        matmuls(2)
+        x3 = open_group("x3", [("x", 3)])
+        w3 = open_group("w3", [("w", 3)])
+        interleave(vector, ("x", 3), 0, HALF)
+        interleave(scalar, ("x", 3), HALF, S)
+        interleave(vector, ("w", 3), 0, 256)
+        interleave(scalar, ("w", 3), 256, M)
+        quantize(x3, [("x", 3)], "x3", "words_x3")
+        quantize(w3, [("w", 3)], "w3", "words_w3", parts=2)
         for m in range(M // P):
             matmul(3, m)
             result = keep.tile([P, S], F32, name=f"result{m}")

@@ -46,17 +46,13 @@ def tile_list_heads_none_kernel(tc, xT, w, wgt, offs, out):
         nc.sync.dma_start(out=weight[:, :HALF], in_=wgt[:, :HALF])
         load_x(0, 0)
         nc.sync.dma_start(out=weight[:, HALF:], in_=wgt[:, HALF:])
-        for a, t in ((0, 1), (0, 2), (0, 3), (1, 0), (1, 1), (1, 2), (1, 3), (2, 0), (2, 1)):
+        for a, t in ((0, 1), (0, 2), (0, 3), (1, 0), (1, 1), (1, 2), (1, 3), (2, 0), (2, 1), (2, 2)):
             load_x(a, t)
-        load_w(0)
-        load_x(2, 2)
-        load_x(2, 3)
-        load_x(3, 0)
-        load_w(1)
-        load_x(3, 1)
-        load_x(3, 2)
         load_w(2)
-        load_x(3, 3)
+        for a, t in ((2, 3), (3, 0), (3, 1), (3, 2), (3, 3)):
+            load_x(a, t)
+        load_w(1)
+        load_w(0)
         load_w(3)
 
         picked, rounded, quantized = {}, {}, {}
@@ -73,11 +69,12 @@ def tile_list_heads_none_kernel(tc, xT, w, wgt, offs, out):
                     MULT,
                 )
 
-        def open_group(label, keys):
-            tile = keep.tile([P, len(keys), S, PACK], BF16, name=f"rounded_{label}", align_bytes=64)
+        def open_group(label, keys, slot=None):
+            tile = keep.tile([P, len(keys) * S, PACK], BF16, name=slot or f"rounded_{label}", align_bytes=64)
+            scales = keep.tile([P, len(keys) * S], U8, name=f"scales_{label}", align_bytes=64)
             for i, key in enumerate(keys):
-                rounded[key] = tile[:, i]
-            return tile
+                rounded[key] = tile[:, i * S : (i + 1) * S, :]
+            return keys, tile, scales
 
         def interleave(copy, key, lo, hi):
             side, a = key
@@ -87,19 +84,20 @@ def tile_list_heads_none_kernel(tc, xT, w, wgt, offs, out):
                 in_=src[:, :, lo:hi].rearrange("p t (c i) -> p c t i", i=4),
             )
 
-        def quantize(tile, keys, label, slot, parts=1):
-            words = keep.tile([P, len(keys), S], U32, name=slot, align_bytes=64)
-            scales = keep.tile([P, len(keys), S], U8, name=f"scales_{label}", align_bytes=64)
-            columns = len(keys) * S
-            for part in range(parts):
-                cols = slice(part * columns // parts, (part + 1) * columns // parts)
-                nc.vector.quantize_mx(
-                    out=words[:].rearrange("p k s -> p (k s)")[:, cols].bitcast(FP8X4),
-                    scales=scales[:].rearrange("p k s -> p (k s)")[:, cols],
-                    in_=tile[:].rearrange("p k s t -> p (k s) t")[:, cols, :].rearrange("p c t -> p (c t)"),
-                )
+        def open_words(group, slot):
+            keys, tile, scales = group
+            words = keep.tile([P, len(keys) * S], U32, name=slot, align_bytes=64)
             for i, key in enumerate(keys):
-                quantized[key] = (words[:, i], scales[:, i])
+                quantized[key] = (words[:, i * S : (i + 1) * S], scales[:, i * S : (i + 1) * S])
+            return words
+
+        def quantize_columns(group, words, lo, hi):
+            keys, tile, scales = group
+            nc.vector.quantize_mx(
+                out=words[:, lo:hi].bitcast(FP8X4),
+                scales=scales[:, lo:hi],
+                in_=tile[:, lo:hi, :].rearrange("p c t -> p (c t)"),
+            )
 
         def matmul(a, m):
             cols = slice(m * P, (m + 1) * P)
@@ -111,7 +109,7 @@ def tile_list_heads_none_kernel(tc, xT, w, wgt, offs, out):
                 lhsT_scale=w_scales[:, cols],
                 rhs=x_words.bitcast(FP8X4),
                 rhs_scale=x_scales,
-                start=(a == 0),
+                start=(a == 2),
                 stop=(a == PASSES - 1),
             )
 
@@ -125,42 +123,51 @@ def tile_list_heads_none_kernel(tc, xT, w, wgt, offs, out):
         x0 = open_group("x0", [("x", 0)])
         interleave(scalar, ("x", 0), 0, HALF)
         interleave(scalar, ("x", 0), HALF, S)
-        gather(1, 0)
-        gather(1, 1)
-        gather(1, 2)
-        quantize(x0, [("x", 0)], "x0", "x1_1")
-        gather(1, 3)
-        x1w0 = open_group("x1w0", [("x", 1), ("w", 0)])
+        for t in range(PACK):
+            gather(1, t)
+        gather(2, 0)
+        x0_words = open_words(x0, "x1_3")
+        quantize_columns(x0, x0_words, 0, S)
+        x1w1 = open_group("x1w1", [("x", 1), ("w", 1)])
         interleave(scalar, ("x", 1), 0, HALF)
         interleave(scalar, ("x", 1), HALF, S)
-        interleave(scalar, ("w", 0), 0, M)
-        for t in range(PACK):
-            gather(2, t)
-        quantize(x1w0, [("x", 1), ("w", 0)], "x1w0", "x2_2")
-        matmuls(0)
-        x2w1 = open_group("x2w1", [("x", 2), ("w", 1)])
+        gather(2, 1)
+        gather(2, 2)
+        gather(2, 3)
+        x2w2 = open_group("x2w2", [("x", 2), ("w", 2)])
+        interleave(scalar, ("w", 2), 0, M)
         interleave(scalar, ("x", 2), 0, HALF)
         interleave(scalar, ("x", 2), HALF, S)
-        interleave(scalar, ("w", 1), 0, M)
-        gather(3, 0)
-        gather(3, 1)
-        gather(3, 2)
-        quantize(x2w1, [("x", 2), ("w", 1)], "x2w1", "x3_2")
-        matmuls(1)
-        w2 = open_group("w2", [("w", 2)])
-        interleave(scalar, ("w", 2), 0, M)
-        gather(3, 3)
-        quantize(w2, [("w", 2)], "w2", "x3_3")
-        matmuls(2)
+        for t in range(PACK):
+            gather(3, t)
         x3 = open_group("x3", [("x", 3)])
-        w3 = open_group("w3", [("w", 3)])
-        interleave(vector, ("x", 3), 0, HALF)
-        interleave(scalar, ("x", 3), HALF, S)
-        interleave(vector, ("w", 3), 0, 256)
+        interleave(scalar, ("x", 3), 0, HALF)
+        interleave(vector, ("w", 1), 256, M)
+        interleave(scalar, ("w", 1), 0, 256)
+        interleave(scalar, ("x", 3), 256, 384)
+        x2w2_words = open_words(x2w2, "x3_3")
+        quantize_columns(x2w2, x2w2_words, 0, S + M)
+        matmuls(2)
+        x1w1_words = open_words(x1w1, "words_x1w1")
+        quantize_columns(x1w1, x1w1_words, 0, S + M)
+        matmuls(1)
+        w0 = open_group("w0", [("w", 0)], "rounded_x2w2")
+        interleave(scalar, ("w", 0), 0, 256)
+        interleave(vector, ("w", 0), 256, M)
+        interleave(vector, ("x", 3), 384, S)
+        w0_words = open_words(w0, "words_w0")
+        quantize_columns(w0, w0_words, 0, M)
+        matmuls(0)
+        w3 = open_group("w3", [("w", 3)], "rounded_x1w1")
+        interleave(vector, ("w", 3), 0, 128)
         interleave(scalar, ("w", 3), 256, M)
-        quantize(x3, [("x", 3)], "x3", "words_x3")
-        quantize(w3, [("w", 3)], "w3", "words_w3", parts=2)
-        for m in range(M // P):
+        interleave(scalar, ("w", 3), 128, 256)
+        x3_words = open_words(x3, "words_x3")
+        quantize_columns(x3, x3_words, 0, S)
+        w3_words = open_words(w3, "words_w3")
+        quantize_columns(w3, w3_words, 256, M)
+        quantize_columns(w3, w3_words, 0, 256)
+        for m in (2, 3, 0, 1):
             matmul(3, m)
             result = keep.tile([P, S], F32, name=f"result{m}")
             if m % 2:

@@ -15,163 +15,159 @@ MULT = mybir.AluOpType.mult
 
 P = 128
 PACK = 4
-PASSES = K // (P * PACK)
-HALF = S // 2
-assert M == S
+K_PASS = P * PACK
+PASSES = K // K_PASS
+PASS_ORDER = (2, 1, 0, 3)
+HALF = 256
+OFFSETS_PER_COLUMN = 16
+RUN = 4
+
+assert S == M == 2 * HALF
 
 
 def tile_list_heads_none_kernel(tc, xT, w, wgt, offs, out):
     nc = tc.nc
+    by_scalar, by_vector = nc.scalar.copy, nc.vector.tensor_copy
+
     with ExitStack() as ctx:
         keep = ctx.enter_context(tc.tile_pool(name="keep", bufs=1))
-        stage = ctx.enter_context(tc.tile_pool(name="stage", bufs=3))
+        gathered = ctx.enter_context(tc.tile_pool(name="gathered", bufs=3))
         psum = ctx.enter_context(tc.psum_pool(name="psum", bufs=1))
 
-        offsets = keep.tile([P, S // 16], U16, name="offsets")
+        offsets = keep.tile([P, S // OFFSETS_PER_COLUMN], U16, name="offsets")
         weight = keep.tile([P, S], F32, name="weight")
-        planes = [[keep.tile([P, T], F32, name=f"x{a}_{t}", align_bytes=64) for t in range(PACK)] for a in range(PASSES)]
-        w_raw = [keep.tile([P, PACK, M], F32, name=f"w{a}") for a in range(PASSES)]
-        acc = [psum.tile([P, S], F32, name=f"acc{m}") for m in range(M // P)]
+        planes = [
+            [keep.tile([P, T], F32, name=f"plane_{a}_{t}", align_bytes=64) for t in range(PACK)]
+            for a in range(PASSES)
+        ]
+        w_rows = [keep.tile([P, PACK, M], F32, name=f"w_rows_{a}") for a in range(PASSES)]
+        sums = [psum.tile([P, S], F32, name=f"sums_{m}") for m in range(M // P)]
 
-        xv = xT.rearrange("(a p t) s -> a t p s", p=P, t=PACK)
-        wv = w.rearrange("(a p t) n -> a p t n", p=P, t=PACK)
+        xT_planes = xT.rearrange("(a p t) s -> a t p s", p=P, t=PACK)
+        w_passes = w.rearrange("(a p t) n -> a p t n", p=P, t=PACK)
 
-        def load_x(a, t):
-            nc.sync.dma_start(out=planes[a][t][:], in_=xv[a, t])
+        def load_planes(*which):
+            for a, t in which:
+                nc.sync.dma_start(out=planes[a][t][:], in_=xT_planes[a, t])
 
         def load_w(a):
-            nc.sync.dma_start(out=w_raw[a][:], in_=wv[a])
+            nc.sync.dma_start(out=w_rows[a][:], in_=w_passes[a])
 
         nc.sync.dma_start(offsets[:], offs)
         nc.sync.dma_start(out=weight[:, :HALF], in_=wgt[:, :HALF])
-        load_x(0, 0)
+        load_planes((0, 0))
         nc.sync.dma_start(out=weight[:, HALF:], in_=wgt[:, HALF:])
-        for a, t in ((0, 1), (0, 2), (0, 3), (1, 0), (1, 1), (1, 2), (1, 3), (2, 0), (2, 1), (2, 2)):
-            load_x(a, t)
+        load_planes((0, 1), (0, 2), (0, 3), (1, 0), (1, 1), (1, 2), (1, 3), (2, 0), (2, 1), (2, 2))
         load_w(2)
-        for a, t in ((2, 3), (3, 0), (3, 1), (3, 2), (3, 3)):
-            load_x(a, t)
+        load_planes((2, 3), (3, 0), (3, 1), (3, 2), (3, 3))
         load_w(1)
         load_w(0)
         load_w(3)
 
-        picked, rounded, quantized = {}, {}, {}
+        products = {}
 
         def gather(a, t):
             if t == 0:
-                picked[a] = stage.tile([P, PACK, S], F32, name="picked")
-            for h in range(2):
-                cols = slice(h * HALF, (h + 1) * HALF)
-                nc.vector.tensor_tensor(
-                    picked[a][:, t, cols],
-                    planes[a][t][:].indirect(offsets[:, h * HALF // 16 : (h + 1) * HALF // 16]),
-                    weight[:, cols],
-                    MULT,
-                )
+                products[a] = gathered.tile([P, PACK, S], F32, name="products")
+            for lo in (0, HALF):
+                cols = slice(lo, lo + HALF)
+                listed = offsets[:, lo // OFFSETS_PER_COLUMN : (lo + HALF) // OFFSETS_PER_COLUMN]
+                nc.vector.tensor_tensor(products[a][:, t, cols], planes[a][t][:].indirect(listed), weight[:, cols], MULT)
 
-        def open_group(label, keys, slot=None):
-            tile = keep.tile([P, len(keys) * S, PACK], BF16, name=slot or f"rounded_{label}", align_bytes=64)
-            scales = keep.tile([P, len(keys) * S], U8, name=f"scales_{label}", align_bytes=64)
-            for i, key in enumerate(keys):
-                rounded[key] = tile[:, i * S : (i + 1) * S, :]
-            return keys, tile, scales
+        def new_values(label, width):
+            return keep.tile([P, width, PACK], BF16, name=f"values_{label}", align_bytes=64)
 
-        def interleave(copy, key, lo, hi):
-            side, a = key
-            src = picked[a] if side == "x" else w_raw[a]
+        def interleave(copy, values, source):
             copy(
-                out=rounded[key][:, lo:hi, :].rearrange("p (c i) t -> p c t i", i=4),
-                in_=src[:, :, lo:hi].rearrange("p t (c i) -> p c t i", i=4),
+                out=values.rearrange("p (c i) t -> p c t i", i=RUN),
+                in_=source.rearrange("p t (c i) -> p c t i", i=RUN),
             )
 
-        def open_words(group, slot):
-            keys, tile, scales = group
-            words = keep.tile([P, len(keys) * S], U32, name=slot, align_bytes=64)
-            for i, key in enumerate(keys):
-                quantized[key] = (words[:, i * S : (i + 1) * S], scales[:, i * S : (i + 1) * S])
-            return words
+        def new_words(label, width, name=None):
+            words = keep.tile([P, width], U32, name=name or f"words_{label}", align_bytes=64)
+            scales = keep.tile([P, width], U8, name=f"scales_{label}", align_bytes=64)
+            return words[:], scales[:]
 
-        def quantize_columns(group, words, lo, hi):
-            keys, tile, scales = group
+        def columns(pair, lo, hi):
+            words, scales = pair
+            return words[:, lo:hi], scales[:, lo:hi]
+
+        def quantise(pair, values):
+            words, scales = pair
             nc.vector.quantize_mx(
-                out=words[:, lo:hi].bitcast(FP8X4),
-                scales=scales[:, lo:hi],
-                in_=tile[:, lo:hi, :].rearrange("p c t -> p (c t)"),
+                out=words.bitcast(FP8X4), scales=scales, in_=values.rearrange("p c t -> p (c t)")
             )
 
-        def matmul(a, m):
-            cols = slice(m * P, (m + 1) * P)
-            w_words, w_scales = quantized["w", a]
-            x_words, x_scales = quantized["x", a]
+        def multiply(a, m, w_pair, x_pair):
+            w_words, w_scales = columns(w_pair, m * P, (m + 1) * P)
+            x_words, x_scales = x_pair
             nc.tensor.matmul_mx(
-                out=acc[m][:],
-                lhsT=w_words[:, cols].bitcast(FP8X4),
-                lhsT_scale=w_scales[:, cols],
+                out=sums[m][:],
+                lhsT=w_words.bitcast(FP8X4),
+                lhsT_scale=w_scales,
                 rhs=x_words.bitcast(FP8X4),
                 rhs_scale=x_scales,
-                start=(a == 2),
-                stop=(a == PASSES - 1),
+                start=(a == PASS_ORDER[0]),
+                stop=(a == PASS_ORDER[-1]),
             )
 
-        def matmuls(a):
+        def multiply_all(a, w_pair, x_pair):
             for m in range(M // P):
-                matmul(a, m)
+                multiply(a, m, w_pair, x_pair)
 
-        scalar, vector = nc.scalar.copy, nc.vector.tensor_copy
         for t in range(PACK):
             gather(0, t)
-        x0 = open_group("x0", [("x", 0)])
-        interleave(scalar, ("x", 0), 0, HALF)
-        interleave(scalar, ("x", 0), HALF, S)
+        x0_values = new_values("x0", S)
+        for lo in (0, HALF):
+            interleave(by_scalar, x0_values[:, lo : lo + HALF, :], products[0][:, :, lo : lo + HALF])
         for t in range(PACK):
             gather(1, t)
         gather(2, 0)
-        x0_words = open_words(x0, "x1_3")
-        quantize_columns(x0, x0_words, 0, S)
-        x1w1 = open_group("x1w1", [("x", 1), ("w", 1)])
-        interleave(scalar, ("x", 1), 0, HALF)
-        interleave(scalar, ("x", 1), HALF, S)
-        gather(2, 1)
-        gather(2, 2)
-        gather(2, 3)
-        x2w2 = open_group("x2w2", [("x", 2), ("w", 2)])
-        interleave(scalar, ("w", 2), 0, M)
-        interleave(scalar, ("x", 2), 0, HALF)
-        interleave(scalar, ("x", 2), HALF, S)
+        x0 = new_words("x0", S, name="plane_1_3")
+        quantise(x0, x0_values[:])
+        x1w1_values = new_values("x1w1", S + M)
+        for lo in (0, HALF):
+            interleave(by_scalar, x1w1_values[:, lo : lo + HALF, :], products[1][:, :, lo : lo + HALF])
+        for t in range(1, PACK):
+            gather(2, t)
+        x2w2_values = new_values("x2w2", S + M)
+        interleave(by_scalar, x2w2_values[:, S:, :], w_rows[2][:])
+        for lo in (0, HALF):
+            interleave(by_scalar, x2w2_values[:, lo : lo + HALF, :], products[2][:, :, lo : lo + HALF])
+
         for t in range(PACK):
             gather(3, t)
-        x3 = open_group("x3", [("x", 3)])
-        interleave(scalar, ("x", 3), 0, HALF)
-        interleave(vector, ("w", 1), 256, M)
-        interleave(scalar, ("w", 1), 0, 256)
-        interleave(scalar, ("x", 3), 256, 384)
-        x2w2_words = open_words(x2w2, "x3_3")
-        quantize_columns(x2w2, x2w2_words, 0, S + M)
-        matmuls(2)
-        x1w1_words = open_words(x1w1, "words_x1w1")
-        quantize_columns(x1w1, x1w1_words, 0, S + M)
-        matmuls(1)
-        w0 = open_group("w0", [("w", 0)], "rounded_x2w2")
-        interleave(scalar, ("w", 0), 0, 256)
-        interleave(vector, ("w", 0), 256, M)
-        interleave(vector, ("x", 3), 384, S)
-        w0_words = open_words(w0, "words_w0")
-        quantize_columns(w0, w0_words, 0, M)
-        matmuls(0)
-        w3 = open_group("w3", [("w", 3)], "rounded_x1w1")
-        interleave(vector, ("w", 3), 0, 128)
-        interleave(scalar, ("w", 3), 256, M)
-        interleave(scalar, ("w", 3), 128, 256)
-        x3_words = open_words(x3, "words_x3")
-        quantize_columns(x3, x3_words, 0, S)
-        w3_words = open_words(w3, "words_w3")
-        quantize_columns(w3, w3_words, 256, M)
-        quantize_columns(w3, w3_words, 0, 256)
+        x3_values = new_values("x3", S)
+        for lo in (0, HALF):
+            interleave(by_scalar, x3_values[:, lo : lo + HALF, :], products[3][:, :, lo : lo + HALF])
+        x2w2 = new_words("x2w2", S + M, name="plane_3_3")
+        quantise(x2w2, x2w2_values[:])
+        multiply_all(2, columns(x2w2, S, S + M), columns(x2w2, 0, S))
+
+        interleave(by_vector, x1w1_values[:, S:, :], w_rows[1][:])
+        w0_values = new_values("w0", M)
+        interleave(by_scalar, w0_values[:], w_rows[0][:])
+        x1w1 = new_words("x1w1", S + M)
+        quantise(x1w1, x1w1_values[:])
+        multiply_all(1, columns(x1w1, S, S + M), columns(x1w1, 0, S))
+
+        x3 = new_words("x3", S)
+        quantise(x3, x3_values[:])
+        w0 = new_words("w0", M)
+        quantise(w0, w0_values[:])
+        multiply_all(0, w0, x0)
+
+        w3 = new_words("w3", M)
+        halves = [(by_scalar, HALF, M), (by_vector, 0, HALF)]
+        half_values = [new_values(f"w3_{lo}", HALF) for copy, lo, hi in halves]
+        for values, (copy, lo, hi) in zip(half_values, halves):
+            interleave(copy, values[:], w_rows[3][:, :, lo:hi])
+        for values, (copy, lo, hi) in zip(half_values, halves):
+            quantise(columns(w3, lo, hi), values[:])
+            for m in range(lo // P, hi // P):
+                multiply(3, m, w3, x3)
         for m in (2, 3, 0, 1):
-            matmul(3, m)
-            result = keep.tile([P, S], F32, name=f"result{m}")
-            if m % 2:
-                nc.scalar.copy(out=result[:], in_=acc[m][:])
-            else:
-                nc.vector.tensor_copy(out=result[:], in_=acc[m][:])
+            result = keep.tile([P, S], F32, name=f"result_{m}")
+            copy = by_scalar if m % 2 else by_vector
+            copy(out=result[:], in_=sums[m][:])
             nc.sync.dma_start(out=out[m * P : (m + 1) * P, :], in_=result[:])

from contextlib import ExitStack

import concourse.mybir as mybir

K, M, T, S = 2048, 512, 1024, 512
FLOPS = 2 * K * M * S

F32 = mybir.dt.float32
BF16 = mybir.dt.bfloat16
U32 = mybir.dt.uint32
U16 = mybir.dt.uint16
U8 = mybir.dt.uint8
FP8X4 = mybir.dt.float8_e4m3fn_x4
MULT = mybir.AluOpType.mult

P = 128
PACK = 4
K_PASS = P * PACK
PASSES = K // K_PASS
PASS_ORDER = (2, 1, 0, 3)
HALF = 256
OFFSETS_PER_COLUMN = 16
RUN = 4

assert S == M == 2 * HALF


def tile_list_heads_none_kernel(tc, xT, w, wgt, offs, out):
    nc = tc.nc
    by_scalar, by_vector = nc.scalar.copy, nc.vector.tensor_copy

    with ExitStack() as ctx:
        keep = ctx.enter_context(tc.tile_pool(name="keep", bufs=1))
        gathered = ctx.enter_context(tc.tile_pool(name="gathered", bufs=3))
        psum = ctx.enter_context(tc.psum_pool(name="psum", bufs=1))

        offsets = keep.tile([P, S // OFFSETS_PER_COLUMN], U16, name="offsets")
        weight = keep.tile([P, S], F32, name="weight")
        planes = [
            [keep.tile([P, T], F32, name=f"plane_{a}_{t}", align_bytes=64) for t in range(PACK)]
            for a in range(PASSES)
        ]
        w_rows = [keep.tile([P, PACK, M], F32, name=f"w_rows_{a}") for a in range(PASSES)]
        sums = [psum.tile([P, S], F32, name=f"sums_{m}") for m in range(M // P)]

        xT_planes = xT.rearrange("(a p t) s -> a t p s", p=P, t=PACK)
        w_passes = w.rearrange("(a p t) n -> a p t n", p=P, t=PACK)

        def load_planes(*which):
            for a, t in which:
                nc.sync.dma_start(out=planes[a][t][:], in_=xT_planes[a, t])

        def load_w(a):
            nc.sync.dma_start(out=w_rows[a][:], in_=w_passes[a])

        nc.sync.dma_start(offsets[:], offs)
        nc.sync.dma_start(out=weight[:, :HALF], in_=wgt[:, :HALF])
        load_planes((0, 0))
        nc.sync.dma_start(out=weight[:, HALF:], in_=wgt[:, HALF:])
        load_planes((0, 1), (0, 2), (0, 3), (1, 0), (1, 1), (1, 2), (1, 3), (2, 0), (2, 1), (2, 2))
        load_w(2)
        load_planes((2, 3), (3, 0), (3, 1), (3, 2), (3, 3))
        load_w(1)
        load_w(0)
        load_w(3)

        products = {}

        def gather(a, t):
            if t == 0:
                products[a] = gathered.tile([P, PACK, S], F32, name="products")
            for lo in (0, HALF):
                cols = slice(lo, lo + HALF)
                listed = offsets[:, lo // OFFSETS_PER_COLUMN : (lo + HALF) // OFFSETS_PER_COLUMN]
                nc.vector.tensor_tensor(products[a][:, t, cols], planes[a][t][:].indirect(listed), weight[:, cols], MULT)

        def new_values(label, width):
            return keep.tile([P, width, PACK], BF16, name=f"values_{label}", align_bytes=64)

        def interleave(copy, values, source):
            copy(
                out=values.rearrange("p (c i) t -> p c t i", i=RUN),
                in_=source.rearrange("p t (c i) -> p c t i", i=RUN),
            )

        def new_words(label, width, name=None):
            words = keep.tile([P, width], U32, name=name or f"words_{label}", align_bytes=64)
            scales = keep.tile([P, width], U8, name=f"scales_{label}", align_bytes=64)
            return words[:], scales[:]

        def columns(pair, lo, hi):
            words, scales = pair
            return words[:, lo:hi], scales[:, lo:hi]

        def quantise(pair, values):
            words, scales = pair
            nc.vector.quantize_mx(
                out=words.bitcast(FP8X4), scales=scales, in_=values.rearrange("p c t -> p (c t)")
            )

        def multiply(a, m, w_pair, x_pair):
            w_words, w_scales = columns(w_pair, m * P, (m + 1) * P)
            x_words, x_scales = x_pair
            nc.tensor.matmul_mx(
                out=sums[m][:],
                lhsT=w_words.bitcast(FP8X4),
                lhsT_scale=w_scales,
                rhs=x_words.bitcast(FP8X4),
                rhs_scale=x_scales,
                start=(a == PASS_ORDER[0]),
                stop=(a == PASS_ORDER[-1]),
            )

        def multiply_all(a, w_pair, x_pair):
            for m in range(M // P):
                multiply(a, m, w_pair, x_pair)

        for t in range(PACK):
            gather(0, t)
        x0_values = new_values("x0", S)
        for lo in (0, HALF):
            interleave(by_scalar, x0_values[:, lo : lo + HALF, :], products[0][:, :, lo : lo + HALF])
        for t in range(PACK):
            gather(1, t)
        gather(2, 0)
        x0 = new_words("x0", S, name="plane_1_3")
        quantise(x0, x0_values[:])
        x1w1_values = new_values("x1w1", S + M)
        for lo in (0, HALF):
            interleave(by_scalar, x1w1_values[:, lo : lo + HALF, :], products[1][:, :, lo : lo + HALF])
        for t in range(1, PACK):
            gather(2, t)
        x2w2_values = new_values("x2w2", S + M)
        interleave(by_scalar, x2w2_values[:, S:, :], w_rows[2][:])
        for lo in (0, HALF):
            interleave(by_scalar, x2w2_values[:, lo : lo + HALF, :], products[2][:, :, lo : lo + HALF])

        for t in range(PACK):
            gather(3, t)
        x3_values = new_values("x3", S)
        for lo in (0, HALF):
            interleave(by_scalar, x3_values[:, lo : lo + HALF, :], products[3][:, :, lo : lo + HALF])
        x2w2 = new_words("x2w2", S + M, name="plane_3_3")
        quantise(x2w2, x2w2_values[:])
        multiply_all(2, columns(x2w2, S, S + M), columns(x2w2, 0, S))

        interleave(by_vector, x1w1_values[:, S:, :], w_rows[1][:])
        w0_values = new_values("w0", M)
        interleave(by_scalar, w0_values[:], w_rows[0][:])
        x1w1 = new_words("x1w1", S + M)
        quantise(x1w1, x1w1_values[:])
        multiply_all(1, columns(x1w1, S, S + M), columns(x1w1, 0, S))

        x3 = new_words("x3", S)
        quantise(x3, x3_values[:])
        w0 = new_words("w0", M)
        quantise(w0, w0_values[:])
        multiply_all(0, w0, x0)

        w3 = new_words("w3", M)
        halves = [(by_scalar, HALF, M), (by_vector, 0, HALF)]
        half_values = [new_values(f"w3_{lo}", HALF) for copy, lo, hi in halves]
        for values, (copy, lo, hi) in zip(half_values, halves):
            interleave(copy, values[:], w_rows[3][:, :, lo:hi])
        for values, (copy, lo, hi) in zip(half_values, halves):
            quantise(columns(w3, lo, hi), values[:])
            for m in range(lo // P, hi // P):
                multiply(3, m, w3, x3)
        for m in (2, 3, 0, 1):
            result = keep.tile([P, S], F32, name=f"result_{m}")
            copy = by_scalar if m % 2 else by_vector
            copy(out=result[:], in_=sums[m][:])
            nc.sync.dma_start(out=out[m * P : (m + 1) * P, :], in_=result[:])
